import numpy as np
import ml_dtypes


def mxq(x, axis, fmt="e4m3"):
    dtype, down = {"e4m3": (ml_dtypes.float8_e4m3fn, 7), "e5m2": (ml_dtypes.float8_e5m2, 14)}[fmt]
    v = np.moveaxis(np.asarray(x, np.float32).astype(ml_dtypes.bfloat16).astype(np.float64), axis, -1)
    blocks = v.reshape(v.shape[:-1] + (-1, 32))
    amax = np.abs(blocks).max(-1, keepdims=True)
    byte = np.maximum(np.where(amax > 0, np.frexp(amax)[1] - 1 + 127, 0) - down, 1)
    scale = np.exp2(byte - 127.0)
    codes = (blocks / scale).astype(np.float32).astype(dtype).astype(np.float64)
    return np.moveaxis((codes * scale).reshape(v.shape), -1, axis)


WIDE = False


def mx_kscale(k):
    if not WIDE:
        return np.ones(k)
    levels = np.array([10, -10, 5, -5, 0])
    if k % 512:
        return np.exp2(np.random.permutation(np.resize(levels, k // 32))).repeat(32)
    a = np.empty((k // 512, 16))
    for p in range(k // 512):
        a[p, :8] = np.random.permutation(np.resize(levels, 8))
        for g in range(8):
            far = levels[np.abs(levels - a[p, g]) >= 10]
            a[p, g + 8] = far[np.random.randint(len(far))]
    return np.exp2(a.ravel()).repeat(32)


def f64(x):
    return np.asarray(x).astype(np.float64)


def striped(idx):
    return np.tile(idx.reshape(-1, 16).T, (8, 1)).astype(np.uint16)


def unstriped(offs):
    return offs[:16].T.reshape(-1).astype(np.int64)


def striped8(idx):
    return np.concatenate([x.reshape(-1, 16).T for x in idx]).astype(np.uint16)


def runs(offs, k):
    lists = np.stack([offs[16 * r : 16 * r + 16].T.reshape(-1) for r in range(8)]).astype(np.int64)
    return lists[np.arange(k) % 512 // 64]


def pack_weight(w):
    k, n = w.shape
    w = f64(np.asarray(w, np.float32).astype(ml_dtypes.bfloat16)).reshape(k // 32, 32, n)
    amax = np.abs(w).max(1)
    byte = np.clip(np.where(amax > 0, np.frexp(amax)[1] - 1 + 127 - 7, 1), 1, 254)
    scaled = (w * np.exp2(127.0 - byte)[:, None, :]).reshape(k, n).astype(np.float32)
    words = np.ascontiguousarray(scaled.reshape(k // 512, 128, 4, n).transpose(0, 1, 3, 2)).astype(ml_dtypes.float8_e4m3fn).view(np.uint8)
    return words, np.ascontiguousarray(byte.astype(np.uint8).reshape(k // 512, 16, n))


def unpack_weight(words, scales):
    g, p, n, _ = words.shape
    vals = np.ascontiguousarray(words).view(ml_dtypes.float8_e4m3fn).astype(np.float64) * np.repeat(np.exp2(scales.astype(np.float64) - 127.0), 8, axis=1)[..., None]
    return vals.transpose(0, 1, 3, 2).reshape(g * 512, n)


def sigmoid(v):
    return 1.0 / (1.0 + np.exp(-np.maximum(v, -700.0)))

def planes(y):
    n, m = y.shape
    v = y.astype(np.float32).astype(ml_dtypes.bfloat16).astype(np.float64).reshape(n // 32, 32, m)
    top = np.abs(v).max(1)
    byte = np.clip(np.where(top > 0, np.frexp(top)[1] - 1 + 127 - 7, 1), 1, 254)
    codes = (v * np.exp2(127.0 - byte)[:, None, :]).reshape(n, m).astype(np.float32).astype(ml_dtypes.float8_e4m3fn).view(np.uint8)
    words = codes.reshape(n // 512, 128, 4, m).transpose(0, 1, 3, 2)
    return np.ascontiguousarray(words), np.ascontiguousarray(byte.astype(np.uint8).reshape(n // 512, 16, m))


K, T, S, G, H, U = 512, 1024, 256, 2048, 512, 512


def setup_inputs():
    n = np.random.standard_normal
    s = mx_kscale(K)[:, None]
    packed_xT = pack_weight(n((K, T)) * s)
    packed_dT = pack_weight(n((K, G)) / s)
    perm = np.random.permutation(U)
    return {
        "x_words": packed_xT[0],
        "x_scales": packed_xT[1],
        "d_words": packed_dT[0],
        "d_scales": packed_dT[1],
        "sl": np.random.uniform(1.0, 2.0, (H, 1)).astype(np.float32),
        "th": (0.5 * n((H, 1))).astype(np.float32),
        "gs": (np.random.uniform(0.5, 1.5, (K, 1)) * s).astype(np.float32),
        "offs": striped8(np.random.randint(0, T, (8, S))),
        "ka": striped8(np.random.randint(0, G, (8, H))),
        "kb": striped8(np.random.randint(0, G, (8, H))),
        "n1": striped(np.random.permutation(S)),
        "n2": striped(np.random.permutation(S)),
        "k1": striped8(np.random.randint(0, G, (8, H))),
        "k2": striped8(np.random.randint(0, G, (8, H))),
        "two": striped(np.random.permutation(T)[:S]),
        "k3": striped8(np.random.randint(0, G, (8, H))),
        "hz": striped8(np.random.randint(0, T, (8, S))),
        "n3": striped(perm[:S]),
        "n4": striped(perm[S:]),
        "n5": striped(np.random.permutation(S)),
    }


def reference(x_words, x_scales, d_words, d_scales, sl, th, gs, offs, ka, kb, n1, n2, k1, k2, two, k3, hz, n3, n4, n5):
    d_k1 = unpack_weight(d_words, d_scales)[np.arange(K)[:, None], runs(k1, K)]
    d_ka = unpack_weight(d_words, d_scales)[np.arange(K)[:, None], runs(ka, K)]
    xq = unpack_weight(x_words, x_scales)[np.arange(K)[:, None], runs(offs, K)]
    d_kb = unpack_weight(d_words, d_scales)[np.arange(K)[:, None], runs(kb, K)]
    h = 0.0625 * (d_ka.T @ xq + d_kb.T @ xq)
    ds = np.zeros((H, S))
    ds[:, unstriped(n1)] = h
    sg = sigmoid(f64(sl) * (h[:, unstriped(n2)] - f64(th)))
    z = f64(gs) * (ds * sg)
    d_k2 = unpack_weight(d_words, d_scales)[np.arange(K)[:, None], runs(k2, K)]
    x_two = unpack_weight(x_words, x_scales)[:, unstriped(two)]
    d_k3 = unpack_weight(d_words, d_scales)[np.arange(K)[:, None], runs(k3, K)]
    x_hz = unpack_weight(x_words, x_scales)[np.arange(K)[:, None], runs(hz, K)]
    h2 = 0.0625 * ((d_k1.T @ mxq(z, 0, "e4m3") + d_k2.T @ x_two + d_k3.T @ x_hz))
    ds2 = np.zeros((H, S))
    ds2[:, unstriped(n5)] = h2
    up = np.maximum(h2, ds2)
    ph = np.zeros((H, U))
    ph[:, unstriped(n3)] = ds2
    out = ph.copy()
    out[:, unstriped(n4)] = up
    return (out,) + planes(out)

@@ -1,0 +1,201 @@
+from contextlib import ExitStack
+
+import concourse.mybir as mybir
+
+K, T, S, G, H, U = 512, 1024, 256, 2048, 512, 512
+FLOPS = 5 * 2 * K * H * S
+
+F32 = mybir.dt.float32
+BF16 = mybir.dt.bfloat16
+I32 = mybir.dt.int32
+U32 = mybir.dt.uint32
+U16 = mybir.dt.uint16
+U8 = mybir.dt.uint8
+FP8X4 = mybir.dt.float8_e4m3fn_x4
+ACT = mybir.ActivationFunctionType
+ALU = mybir.AluOpType
+
+P = 128
+PACK = 4
+HALF = S // 2
+DS_WIDTH = 352
+
+
+def tile_picked_ahzmthesndpagsn_none_po_kernel(tc, x_words, x_scales, d_words, d_scales, sl, th, gs, offs, ka, kb, n1, n2, k1, k2, two, k3, hz, n3, n4, n5, out_0, out_1, out_2):
+    nc = tc.nc
+    with ExitStack() as ctx:
+        lists = ctx.enter_context(tc.tile_pool(name="lists", bufs=1))
+        keep = ctx.enter_context(tc.tile_pool(name="keep", bufs=1))
+        psum = ctx.enter_context(tc.psum_pool(name="psum", bufs=1))
+
+        def load_list(name, dram):
+            tile = lists.tile(list(dram.shape), U16, name="list_" + name)
+            nc.sync.dma_start(tile[:], dram)
+            return tile
+
+        d_bytes = keep.tile([P, G], U8, name="d_bytes")
+        x_bytes = keep.tile([P, T], U8, name="x_bytes")
+        nc.vector.memset(d_bytes[:].bitcast(I32), 0)
+        nc.gpsimd.memset(x_bytes[:].bitcast(I32), 0)
+        nc.scalar.dma_start(d_bytes[0:P:8, :].bitcast(I32), d_scales[0].bitcast(I32))
+        nc.scalar.dma_start(x_bytes[0:P:8, :].bitcast(I32), x_scales[0].bitcast(I32))
+
+        l_ka = load_list("ka", ka)
+        l_offs = load_list("offs", offs)
+        l_kb = load_list("kb", kb)
+        l_n1 = load_list("n1", n1)
+        x_table = keep.tile([P, T], U32, name="x_table")
+        d_table = keep.tile([P, G], U32, name="d_table")
+        nc.sync.dma_start(x_table[:].bitcast(I32), x_words[0].rearrange("p c r -> p (c r)").bitcast(I32))
+        nc.sync.dma_start(d_table[:].bitcast(I32), d_words[0].rearrange("p c r -> p (c r)").bitcast(I32))
+        l_n2 = load_list("n2", n2)
+        l_k2 = load_list("k2", k2)
+        l_k3 = load_list("k3", k3)
+        l_k1 = load_list("k1", k1)
+        l_two = load_list("two", two)
+        l_hz = load_list("hz", hz)
+        l_n5 = load_list("n5", n5)
+        l_n3 = load_list("n3", n3)
+        l_n4 = load_list("n4", n4)
+
+        slope = keep.tile([P, PACK], F32, name="slope")
+        thresh = keep.tile([P, PACK], F32, name="thresh")
+        gain = keep.tile([P, PACK], F32, name="gain")
+        for tile, dram in ((slope, sl), (thresh, th), (gain, gs)):
+            nc.gpsimd.dma_start(tile[:], dram.rearrange("(p t) o -> p (t o)", t=PACK))
+
+        plane1 = keep.tile([P, 2 * H + S], U8, name="plane1", align_bytes=64)
+        plane2 = keep.tile([P, 3 * H + 2 * S], U8, name="plane2", align_bytes=64)
+        nc.vector.memset(plane1[:].bitcast(I32), 0)
+        nc.vector.memset(plane2[:].bitcast(I32), 0)
+        page = [keep.tile([P, U], F32, name=f"page{t}") for t in range(PACK)]
+        for t in range(PACK):
+            nc.vector.memset(page[t][:], 0.0)
+
+        def gather(dst, table, offsets):
+            nc.vector.tensor_copy(dst, table[:].indirect(offsets))
+
+        def move_rows(plane, picked, queues):
+            for a in range(PACK):
+                queues[a % len(queues)].dma_start(plane[a:P:32, :].bitcast(I32), picked[8 * a : P : 32, :].bitcast(I32))
+
+        def deal(dst, raw, n, line):
+            nc.vector.tensor_copy(
+                dst.rearrange("p (l t m i) -> p l m t i", l=n, t=PACK, i=line),
+                raw.rearrange("p (l m i t) -> p l m t i", l=n, t=PACK, i=line),
+            )
+
+        picked1 = keep.tile([P, 2 * H + S], U8, name="picked1")
+        gather(picked1[:, 0:H], d_bytes, l_ka[:])
+        gather(picked1[:, 2 * H :], x_bytes, l_offs[:])
+        gather(picked1[:, H : 2 * H], d_bytes, l_kb[:])
+        dealt1 = keep.tile([P, 2 * H + S], U8, name="dealt1")
+        deal(dealt1[:, 0 : 2 * H], picked1[:, 0 : 2 * H], 2, 16)
+        nc.vector.tensor_copy(dealt1[:, 2 * H :].bitcast(I32), picked1[:, 2 * H :].bitcast(I32))
+        move_rows(plane1, dealt1, (nc.sync, nc.scalar))
+
+        xq = keep.tile([P, S], U32, name="xq", align_bytes=64)
+        gather(xq[:], x_table, l_offs[:])
+        raw1 = keep.tile([P, 2 * H], U32, name="raw1", tag="reused", align_bytes=64)
+        w1 = keep.tile([P, 2 * H], U32, name="w1", align_bytes=64)
+        gather(raw1[:, 0:H], d_table, l_ka[:])
+        gather(raw1[:, H:], d_table, l_kb[:])
+        deal(w1[:], raw1[:], 2, 4)
+
+        bias = keep.tile([P, PACK], F32, name="bias")
+        product = keep.tile([P, PACK], F32, name="product")
+        nc.gpsimd.tensor_tensor(product[:], slope[:], thresh[:], ALU.mult)
+        nc.gpsimd.tensor_scalar(bias[:], product[:], -1.0, 0.0, ALU.mult, ALU.add)
+
+        def mx(acc, w, s, col, rhs, rhs_scale, start, stop):
+            nc.tensor.matmul_mx(acc, lhsT=w[:, col : col + P].bitcast(FP8X4), lhsT_scale=s[:, col : col + P], rhs=rhs.bitcast(FP8X4), rhs_scale=rhs_scale, start=start, stop=stop)
+
+        h, ds = [], []
+        sg = [keep.tile([P, PACK, HALF], F32, name=f"sg{u}") for u in range(2)]
+        for t in range(PACK):
+            acc = psum.tile([P, S], F32, name=f"acc_h{t}", tag=f"bank{t}")
+            for l in range(2):
+                mx(acc[:], w1, plane1, l * H + t * P, xq[:], plane1[:, 2 * H :], l == 0, l == 1)
+            h.append(keep.tile([P, S], F32, name=f"h{t}"))
+            ds.append(keep.tile([P, DS_WIDTH], F32, name=f"ds{t}"))
+            nc.scalar.activation(h[t][:], acc[:], ACT.Copy, scale=0.0625)
+            nc.scalar.activation(ds[t][:].indirect(l_n1[:]), h[t][:], ACT.Copy)
+            nc.scalar.activation(sg[0][:, t, :], h[t][:].indirect(l_n2[:, 0:8]), ACT.Sigmoid, scale=slope[:, t : t + 1], bias=bias[:, t : t + 1])
+        for t in range(PACK):
+            nc.scalar.activation(sg[1][:, t, :], h[t][:].indirect(l_n2[:, 8:16]), ACT.Sigmoid, scale=slope[:, t : t + 1], bias=bias[:, t : t + 1])
+
+        picked2 = keep.tile([P, 3 * H + 2 * S], U8, name="picked2", tag="reused", align_bytes=64)
+        gather(picked2[:, 0:H], d_bytes, l_k2[:])
+        gather(picked2[:, H : 2 * H], d_bytes, l_k3[:])
+        gather(picked2[:, 2 * H : 3 * H], d_bytes, l_k1[:])
+        gather(picked2[:, 3 * H : 3 * H + S], x_bytes, l_two[:])
+        gather(picked2[:, 3 * H + S :], x_bytes, l_hz[:])
+        dealt2 = keep.tile([P, 3 * H + 2 * S], U8, name="dealt2")
+        deal(dealt2[:, 0 : 3 * H], picked2[:, 0 : 3 * H], 3, 16)
+        nc.vector.tensor_copy(dealt2[:, 3 * H :].bitcast(I32), picked2[:, 3 * H :].bitcast(I32))
+        move_rows(plane2, dealt2, (nc.sync,))
+        raw2 = keep.tile([P, 3 * H + 2 * S], U32, name="raw2", tag="reused", align_bytes=64)
+        w2 = keep.tile([P, 3 * H], U32, name="w2", align_bytes=64)
+        x_two = raw2[:, 3 * H : 3 * H + S]
+        x_hz = raw2[:, 3 * H + S :]
+        gather(raw2[:, 0:H], d_table, l_k2[:])
+        gather(raw2[:, H : 2 * H], d_table, l_k3[:])
+        gather(raw2[:, 2 * H : 3 * H], d_table, l_k1[:])
+        gather(x_two, x_table, l_two[:])
+        gather(x_hz, x_table, l_hz[:])
+        deal(w2[:], raw2[:, 0 : 3 * H], 3, 4)
+
+        h2 = [keep.tile([P, S], F32, name=f"h2_{t}") for t in range(PACK)]
+        ds2 = [keep.tile([P, S], F32, name=f"ds2_{t}") for t in range(PACK)]
+        up = [keep.tile([P, S], F32, name=f"up{t}") for t in range(PACK)]
+        for u in range(2):
+            cols = slice(u * HALF, (u + 1) * HALF)
+            z_planes = keep.tile([P, PACK, HALF], BF16, name=f"z_planes{u}")
+            z_words = keep.tile([P, HALF, PACK], BF16, name=f"z_words{u}", align_bytes=64)
+            z_codes = keep.tile([P, HALF], U32, name=f"z_codes{u}", align_bytes=64)
+            z_scales = keep.tile([P, HALF], U8, name=f"z_scales{u}", align_bytes=64)
+            for t in range(PACK):
+                nc.vector.scalar_tensor_tensor(z_planes[:, t, :], ds[t][:, cols], gain[:, t : t + 1], sg[u][:, t, :], ALU.mult, ALU.mult)
+            nc.vector.tensor_copy(z_words[:], z_planes[:].rearrange("p t c -> p c t"))
+            nc.vector.quantize_mx(out=z_codes[:].bitcast(FP8X4), scales=z_scales[:], in_=z_words[:].rearrange("p c t -> p (c t)"))
+            for t in range(PACK):
+                acc = psum.tile([P, HALF], F32, name=f"acc_h2_{u}_{t}", tag=f"bank{PACK * (1 - u) + t}")
+                mx(acc[:], w2, plane2, t * P, x_two[:, cols], plane2[:, 3 * H + u * HALF : 3 * H + (u + 1) * HALF], True, False)
+                mx(acc[:], w2, plane2, H + t * P, x_hz[:, cols], plane2[:, 3 * H + S + u * HALF : 3 * H + S + (u + 1) * HALF], False, False)
+                mx(acc[:], w2, plane2, 2 * H + t * P, z_codes[:], z_scales[:], False, True)
+                nc.vector.tensor_scalar(h2[t][:, cols], acc[:], 0.0625, None, ALU.mult)
+                if u == 0:
+                    nc.scalar.activation(ds2[t][:].indirect(l_n5[:, 0:8]), h2[t][:, cols], ACT.Copy)
+
+        y_words = [keep.tile([P, U // 2, PACK], BF16, name=f"y_words{u}", align_bytes=64) for u in range(2)]
+        y_codes = keep.tile([P, U], U32, name="y_codes", align_bytes=64)
+        y_scales = keep.tile([P, U], U8, name="y_scales", align_bytes=64)
+        out_rows = out_0.rearrange("(p t) c -> p t c", t=PACK)
+
+        def finish_ds2(t):
+            nc.scalar.activation(ds2[t][:].indirect(l_n5[:, 8:16]), h2[t][:, HALF:], ACT.Copy)
+            nc.vector.tensor_tensor(up[t][:], h2[t][:], ds2[t][:], ALU.max)
+
+        finish_ds2(0)
+        for t in range(PACK):
+            if t + 1 < PACK:
+                finish_ds2(t + 1)
+            nc.scalar.activation(page[t][:].indirect(l_n3[:]), ds2[t][:], ACT.Copy)
+            if t > 0:
+                finish_page(nc, t - 1, page, l_n4, up, y_words, out_rows, nc.sync)
+        finish_page(nc, PACK - 1, page, l_n4, up, y_words, out_rows, nc.scalar)
+
+        codes_out = out_1[0].rearrange("p c r -> p (c r)").bitcast(I32)
+        for u in range(2):
+            cols = slice(u * U // 2, (u + 1) * U // 2)
+            nc.vector.quantize_mx(out=y_codes[:, cols].bitcast(FP8X4), scales=y_scales[:, cols], in_=y_words[u][:].rearrange("p c t -> p (c t)"))
+            nc.sync.dma_start(codes_out[:, cols], y_codes[:, cols].bitcast(I32))
+        for q in range(4):
+            (nc.scalar, nc.sync)[q % 2].dma_start(out_2[0][4 * q : 4 * q + 4, :].bitcast(I32), y_scales[32 * q : 32 * q + 4, :].bitcast(I32))
+
+
+def finish_page(nc, t, page, l_n4, up, y_words, out_rows, queue):
+    nc.scalar.activation(page[t][:].indirect(l_n4[:]), up[t][:], ACT.Copy)
+    queue.dma_start(out_rows[:, t, :], page[t][:])
+    for u in range(2):
+        nc.vector.tensor_copy(y_words[u][:, :, t], page[t][:, u * U // 2 : (u + 1) * U // 2])

@@ -1,6 +1,7 @@
 from contextlib import ExitStack
 
 import concourse.mybir as mybir
+from concourse.masks import make_identity
 
 K, T, S, G, H, U = 512, 1024, 256, 2048, 512, 512
 FLOPS = 5 * 2 * K * H * S
@@ -35,19 +36,18 @@ def tile_picked_ahzmthesndpagsn_none_po_kernel(tc, x_words, x_scales, d_words, d
 
         d_bytes = keep.tile([P, G], U8, name="d_bytes")
         x_bytes = keep.tile([P, T], U8, name="x_bytes")
-        nc.vector.memset(d_bytes[:].bitcast(I32), 0)
-        nc.gpsimd.memset(x_bytes[:].bitcast(I32), 0)
-        nc.scalar.dma_start(d_bytes[0:P:8, :].bitcast(I32), d_scales[0].bitcast(I32))
-        nc.scalar.dma_start(x_bytes[0:P:8, :].bitcast(I32), x_scales[0].bitcast(I32))
+        for tile, dram in ((d_bytes, d_scales), (x_bytes, x_scales)):
+            rows = dram[0].bitcast(I32)
+            nc.scalar.dma_start(tile[:].bitcast(I32), rows.unsqueeze(1).to_broadcast([16, 8, rows.shape[1]]))
 
         l_ka = load_list("ka", ka)
         l_offs = load_list("offs", offs)
         l_kb = load_list("kb", kb)
-        l_n1 = load_list("n1", n1)
         x_table = keep.tile([P, T], U32, name="x_table")
         d_table = keep.tile([P, G], U32, name="d_table")
         nc.sync.dma_start(x_table[:].bitcast(I32), x_words[0].rearrange("p c r -> p (c r)").bitcast(I32))
-        nc.sync.dma_start(d_table[:].bitcast(I32), d_words[0].rearrange("p c r -> p (c r)").bitcast(I32))
+        nc.gpsimd.dma_start(d_table[:].bitcast(I32), d_words[0].rearrange("p c r -> p (c r)").bitcast(I32))
+        l_n1 = load_list("n1", n1)
         l_n2 = load_list("n2", n2)
         l_k2 = load_list("k2", k2)
         l_k3 = load_list("k3", k3)
@@ -64,109 +64,137 @@ def tile_picked_ahzmthesndpagsn_none_po_kernel(tc, x_words, x_scales, d_words, d
         for tile, dram in ((slope, sl), (thresh, th), (gain, gs)):
             nc.gpsimd.dma_start(tile[:], dram.rearrange("(p t) o -> p (t o)", t=PACK))
 
-        plane1 = keep.tile([P, 2 * H + S], U8, name="plane1", align_bytes=64)
+        plane1 = keep.tile([P, H + S], U8, name="plane1", align_bytes=64)
+        plane_b = keep.tile([P, H], U8, name="plane_b", align_bytes=64)
         plane2 = keep.tile([P, 3 * H + 2 * S], U8, name="plane2", align_bytes=64)
         nc.vector.memset(plane1[:].bitcast(I32), 0)
+        nc.vector.memset(plane_b[:].bitcast(I32), 0)
         nc.vector.memset(plane2[:].bitcast(I32), 0)
-        page = [keep.tile([P, U], F32, name=f"page{t}") for t in range(PACK)]
-        for t in range(PACK):
-            nc.vector.memset(page[t][:], 0.0)
 
         def gather(dst, table, offsets):
             nc.vector.tensor_copy(dst, table[:].indirect(offsets))
 
-        def move_rows(plane, picked, queues):
+        def move_rows(plane, picked):
             for a in range(PACK):
-                queues[a % len(queues)].dma_start(plane[a:P:32, :].bitcast(I32), picked[8 * a : P : 32, :].bitcast(I32))
+                nc.sync.dma_start(plane[a:P:32, :].bitcast(I32), picked[8 * a : P : 32, :].bitcast(I32))
 
-        def deal(dst, raw, n, line):
-            nc.vector.tensor_copy(
-                dst.rearrange("p (l t m i) -> p l m t i", l=n, t=PACK, i=line),
-                raw.rearrange("p (l m i t) -> p l m t i", l=n, t=PACK, i=line),
-            )
+        identity = keep.tile([P, P], F32, name="identity")
+        make_identity(nc, identity[:])
 
-        picked1 = keep.tile([P, 2 * H + S], U8, name="picked1")
+        def mx(acc, cols, cols_scale, rows, rows_scale, start, stop):
+            nc.tensor.matmul_mx(acc, lhsT=cols.bitcast(FP8X4), lhsT_scale=cols_scale, rhs=rows.bitcast(FP8X4), rhs_scale=rows_scale, start=start, stop=stop)
+
+        picked1 = keep.tile([P, H + S], U8, name="picked1")
+        picked_b = keep.tile([P, H], U8, name="picked_b")
         gather(picked1[:, 0:H], d_bytes, l_ka[:])
-        gather(picked1[:, 2 * H :], x_bytes, l_offs[:])
-        gather(picked1[:, H : 2 * H], d_bytes, l_kb[:])
-        dealt1 = keep.tile([P, 2 * H + S], U8, name="dealt1")
-        deal(dealt1[:, 0 : 2 * H], picked1[:, 0 : 2 * H], 2, 16)
-        nc.vector.tensor_copy(dealt1[:, 2 * H :].bitcast(I32), picked1[:, 2 * H :].bitcast(I32))
-        move_rows(plane1, dealt1, (nc.sync, nc.scalar))
+        gather(picked1[:, H:], x_bytes, l_offs[:])
+        move_rows(plane1, picked1)
+        gather(picked_b[:], d_bytes, l_kb[:])
+        move_rows(plane_b, picked_b)
 
         xq = keep.tile([P, S], U32, name="xq", align_bytes=64)
+        wa = keep.tile([P, H], U32, name="wa", tag="first", align_bytes=64)
+        wb = keep.tile([P, H], U32, name="wb", align_bytes=64)
         gather(xq[:], x_table, l_offs[:])
-        raw1 = keep.tile([P, 2 * H], U32, name="raw1", tag="reused", align_bytes=64)
-        w1 = keep.tile([P, 2 * H], U32, name="w1", align_bytes=64)
-        gather(raw1[:, 0:H], d_table, l_ka[:])
-        gather(raw1[:, H:], d_table, l_kb[:])
-        deal(w1[:], raw1[:], 2, 4)
+        gather(wa[:], d_table, l_ka[:])
+        for v in range(2):
+            gather(wb[:, v * H // 2 : (v + 1) * H // 2], d_table, l_kb[:, 16 * v : 16 * (v + 1)])
 
         bias = keep.tile([P, PACK], F32, name="bias")
         product = keep.tile([P, PACK], F32, name="product")
         nc.gpsimd.tensor_tensor(product[:], slope[:], thresh[:], ALU.mult)
         nc.gpsimd.tensor_scalar(bias[:], product[:], -1.0, 0.0, ALU.mult, ALU.add)
 
-        def mx(acc, w, s, col, rhs, rhs_scale, start, stop):
-            nc.tensor.matmul_mx(acc, lhsT=w[:, col : col + P].bitcast(FP8X4), lhsT_scale=s[:, col : col + P], rhs=rhs.bitcast(FP8X4), rhs_scale=rhs_scale, start=start, stop=stop)
+        acc1 = [psum.tile([P, H], F32, name=f"acc1_{u}") for u in range(2)]
+        for first, n, words, plane in ((0, H, wa, plane1), (0, H // 2, wb, plane_b), (H // 2, H // 2, wb, plane_b)):
+            for u in range(2):
+                rows = slice(first, first + n)
+                mx(acc1[u][:, rows], xq[:, u * HALF : (u + 1) * HALF], plane1[:, H + u * HALF : H + (u + 1) * HALF], words[:, rows], plane[:, rows], n == H, first > 0)
 
         h, ds = [], []
-        sg = [keep.tile([P, PACK, HALF], F32, name=f"sg{u}") for u in range(2)]
+
+        def gate(sg, t, u):
+            nc.scalar.activation(sg[:, t, :], h[t][:].indirect(l_n2[:, 8 * u : 8 * (u + 1)]), ACT.Sigmoid, scale=slope[:, t : t + 1], bias=bias[:, t : t + 1])
+
+        sg0 = keep.tile([P, PACK, HALF], F32, name="sg0", tag="sg")
+        late = [keep.tile([P, 2, P], F32, name=f"late{u}") for u in range(2)]
         for t in range(PACK):
-            acc = psum.tile([P, S], F32, name=f"acc_h{t}", tag=f"bank{t}")
-            for l in range(2):
-                mx(acc[:], w1, plane1, l * H + t * P, xq[:], plane1[:, 2 * H :], l == 0, l == 1)
+            turned = psum.tile([P, S], F32, name=f"turned{t}", tag=f"turn{t}")
+            for u in range(2):
+                dealt = acc1[u][:].rearrange("j (p t) -> j t p", t=PACK)
+                if t < 2:
+                    early = keep.tile([P, P], F32, name=f"early{u}_{t}", tag=f"early{u}_{t}", align_bytes=64)
+                    nc.scalar.copy(early[:], dealt[:, t, :])
+                    src = early[:]
+                else:
+                    if t == 2:
+                        nc.vector.tensor_copy(late[u][:], dealt[:, 2:4, :])
+                    src = late[u][:, t - 2, :]
+                nc.tensor.transpose(turned[:, u * HALF : (u + 1) * HALF], src, identity[:])
             h.append(keep.tile([P, S], F32, name=f"h{t}"))
             ds.append(keep.tile([P, DS_WIDTH], F32, name=f"ds{t}"))
-            nc.scalar.activation(h[t][:], acc[:], ACT.Copy, scale=0.0625)
+            nc.scalar.activation(h[t][:], turned[:], ACT.Copy, scale=0.0625)
+            if t > 0:
+                gate(sg0, t - 1, 0)
+            if t == PACK - 1:
+                gate(sg0, t, 0)
             nc.scalar.activation(ds[t][:].indirect(l_n1[:]), h[t][:], ACT.Copy)
-            nc.scalar.activation(sg[0][:, t, :], h[t][:].indirect(l_n2[:, 0:8]), ACT.Sigmoid, scale=slope[:, t : t + 1], bias=bias[:, t : t + 1])
-        for t in range(PACK):
-            nc.scalar.activation(sg[1][:, t, :], h[t][:].indirect(l_n2[:, 8:16]), ACT.Sigmoid, scale=slope[:, t : t + 1], bias=bias[:, t : t + 1])
 
-        picked2 = keep.tile([P, 3 * H + 2 * S], U8, name="picked2", tag="reused", align_bytes=64)
+        picked2 = keep.tile([P, 3 * H + 2 * S], U8, name="picked2", tag="first", align_bytes=64)
         gather(picked2[:, 0:H], d_bytes, l_k2[:])
         gather(picked2[:, H : 2 * H], d_bytes, l_k3[:])
         gather(picked2[:, 2 * H : 3 * H], d_bytes, l_k1[:])
         gather(picked2[:, 3 * H : 3 * H + S], x_bytes, l_two[:])
         gather(picked2[:, 3 * H + S :], x_bytes, l_hz[:])
-        dealt2 = keep.tile([P, 3 * H + 2 * S], U8, name="dealt2")
-        deal(dealt2[:, 0 : 3 * H], picked2[:, 0 : 3 * H], 3, 16)
-        nc.vector.tensor_copy(dealt2[:, 3 * H :].bitcast(I32), picked2[:, 3 * H :].bitcast(I32))
-        move_rows(plane2, dealt2, (nc.sync,))
-        raw2 = keep.tile([P, 3 * H + 2 * S], U32, name="raw2", tag="reused", align_bytes=64)
-        w2 = keep.tile([P, 3 * H], U32, name="w2", align_bytes=64)
-        x_two = raw2[:, 3 * H : 3 * H + S]
-        x_hz = raw2[:, 3 * H + S :]
-        gather(raw2[:, 0:H], d_table, l_k2[:])
-        gather(raw2[:, H : 2 * H], d_table, l_k3[:])
-        gather(raw2[:, 2 * H : 3 * H], d_table, l_k1[:])
-        gather(x_two, x_table, l_two[:])
-        gather(x_hz, x_table, l_hz[:])
-        deal(w2[:], raw2[:, 0 : 3 * H], 3, 4)
+        move_rows(plane2, picked2)
+        words2 = keep.tile([P, 3 * H + 2 * S], U32, name="words2", tag="early1_1", align_bytes=64)
+        gather(words2[:, 3 * H : 3 * H + S], x_table, l_two[:])
+        gather(words2[:, 0:H], d_table, l_k2[:])
+        gather(words2[:, 3 * H + S :], x_table, l_hz[:])
+        gather(words2[:, H : 2 * H], d_table, l_k3[:])
+        gather(words2[:, 2 * H : 3 * H], d_table, l_k1[:])
+
+        acc2 = [psum.tile([P, H], F32, name=f"acc2_{u}") for u in range(2)]
+        for l in range(2):
+            for u in range(2):
+                x_cols = slice(3 * H + l * S + u * HALF, 3 * H + l * S + (u + 1) * HALF)
+                d_cols = slice(l * H, (l + 1) * H)
+                mx(acc2[u][:], words2[:, x_cols], plane2[:, x_cols], words2[:, d_cols], plane2[:, d_cols], l == 0, False)
 
         h2 = [keep.tile([P, S], F32, name=f"h2_{t}") for t in range(PACK)]
         ds2 = [keep.tile([P, S], F32, name=f"ds2_{t}") for t in range(PACK)]
         up = [keep.tile([P, S], F32, name=f"up{t}") for t in range(PACK)]
         for u in range(2):
             cols = slice(u * HALF, (u + 1) * HALF)
-            z_planes = keep.tile([P, PACK, HALF], BF16, name=f"z_planes{u}")
-            z_words = keep.tile([P, HALF, PACK], BF16, name=f"z_words{u}", align_bytes=64)
+            if u == 0:
+                sg = sg0
+            else:
+                sg = keep.tile([P, PACK, HALF], F32, name="sg1", tag="sg")
+                for t in range(PACK):
+                    gate(sg, t, u)
+            z_planes = keep.tile([P, PACK, HALF], BF16, name=f"z_planes{u}", tag=("z_planes", "z_words")[u], align_bytes=64)
+            z_words = keep.tile([P, HALF, PACK], BF16, name=f"z_words{u}", tag=("z_words", "rows0_0")[u], align_bytes=64)
             z_codes = keep.tile([P, HALF], U32, name=f"z_codes{u}", align_bytes=64)
             z_scales = keep.tile([P, HALF], U8, name=f"z_scales{u}", align_bytes=64)
             for t in range(PACK):
-                nc.vector.scalar_tensor_tensor(z_planes[:, t, :], ds[t][:, cols], gain[:, t : t + 1], sg[u][:, t, :], ALU.mult, ALU.mult)
+                nc.vector.scalar_tensor_tensor(z_planes[:, t, :], ds[t][:, cols], gain[:, t : t + 1], sg[:, t, :], ALU.mult, ALU.mult)
             nc.vector.tensor_copy(z_words[:], z_planes[:].rearrange("p t c -> p c t"))
             nc.vector.quantize_mx(out=z_codes[:].bitcast(FP8X4), scales=z_scales[:], in_=z_words[:].rearrange("p c t -> p (c t)"))
+            d_cols = slice(2 * H, 3 * H)
+            mx(acc2[u][:], z_codes[:], z_scales[:], words2[:, d_cols], plane2[:, d_cols], False, True)
+            dealt = acc2[u][:].rearrange("j (p t) -> j t p", t=PACK)
             for t in range(PACK):
-                acc = psum.tile([P, HALF], F32, name=f"acc_h2_{u}_{t}", tag=f"bank{PACK * (1 - u) + t}")
-                mx(acc[:], w2, plane2, t * P, x_two[:, cols], plane2[:, 3 * H + u * HALF : 3 * H + (u + 1) * HALF], True, False)
-                mx(acc[:], w2, plane2, H + t * P, x_hz[:, cols], plane2[:, 3 * H + S + u * HALF : 3 * H + S + (u + 1) * HALF], False, False)
-                mx(acc[:], w2, plane2, 2 * H + t * P, z_codes[:], z_scales[:], False, True)
-                nc.vector.tensor_scalar(h2[t][:, cols], acc[:], 0.0625, None, ALU.mult)
+                rows = keep.tile([P, P], F32, name=f"rows{u}_{t}", tag=f"rows{u}_{t}", align_bytes=64)
+                nc.vector.tensor_copy(rows[:], dealt[:, t, :])
+                turned = psum.tile([P, HALF], F32, name=f"turned2_{u}_{t}", tag=f"turn{t}")
+                nc.tensor.transpose(turned[:], rows[:], identity[:])
+                nc.vector.tensor_scalar(h2[t][:, cols], turned[:], 0.0625, None, ALU.mult)
                 if u == 0:
                     nc.scalar.activation(ds2[t][:].indirect(l_n5[:, 0:8]), h2[t][:, cols], ACT.Copy)
 
+        page = [keep.tile([P, U], F32, name=f"page{t}", tag=f"rows1_{t}", align_bytes=64) for t in range(PACK)]
+        for t in range(PACK):
+            nc.vector.memset(page[t][:], 0.0)
         y_words = [keep.tile([P, U // 2, PACK], BF16, name=f"y_words{u}", align_bytes=64) for u in range(2)]
         y_codes = keep.tile([P, U], U32, name="y_codes", align_bytes=64)
         y_scales = keep.tile([P, U], U8, name="y_scales", align_bytes=64)

@@ -40,6 +40,9 @@ def tile_picked_ahzmthesndpagsn_none_po_kernel(tc, x_words, x_scales, d_words, d
             rows = dram[0].bitcast(I32)
             nc.scalar.dma_start(tile[:].bitcast(I32), rows.unsqueeze(1).to_broadcast([16, 8, rows.shape[1]]))
 
+        warm = keep.tile([P, 2], F32, name="warm")
+        nc.vector.memset(warm[:, 0:1], 0.0)
+        nc.scalar.activation(warm[:, 1:2], warm[:, 0:1], ACT.Sigmoid)
         l_ka = load_list("ka", ka)
         l_offs = load_list("offs", offs)
         l_kb = load_list("kb", kb)

@@ -36,15 +36,15 @@ def tile_picked_ahzmthesndpagsn_none_po_kernel(tc, x_words, x_scales, d_words, d
 
         d_bytes = keep.tile([P, G], U8, name="d_bytes")
         x_bytes = keep.tile([P, T], U8, name="x_bytes")
-        for tile, dram in ((d_bytes, d_scales), (x_bytes, x_scales)):
+        for tile, dram in ((x_bytes, x_scales), (d_bytes, d_scales)):
             rows = dram[0].bitcast(I32)
             nc.scalar.dma_start(tile[:].bitcast(I32), rows.unsqueeze(1).to_broadcast([16, 8, rows.shape[1]]))
 
         warm = keep.tile([P, 2], F32, name="warm")
         nc.vector.memset(warm[:, 0:1], 0.0)
         nc.scalar.activation(warm[:, 1:2], warm[:, 0:1], ACT.Sigmoid)
-        l_ka = load_list("ka", ka)
         l_offs = load_list("offs", offs)
+        l_ka = load_list("ka", ka)
         l_kb = load_list("kb", kb)
         x_table = keep.tile([P, T], U32, name="x_table")
         d_table = keep.tile([P, G], U32, name="d_table")
@@ -78,8 +78,8 @@ def tile_picked_ahzmthesndpagsn_none_po_kernel(tc, x_words, x_scales, d_words, d
             nc.vector.tensor_copy(dst, table[:].indirect(offsets))
 
         def move_rows(plane, picked):
-            for a in range(PACK):
-                nc.sync.dma_start(plane[a:P:32, :].bitcast(I32), picked[8 * a : P : 32, :].bitcast(I32))
+            for q in range(4):
+                nc.sync.dma_start(plane[32 * q : 32 * q + 4, :].bitcast(I32), picked[32 * q : 32 * (q + 1) : 8, :].bitcast(I32))
 
         identity = keep.tile([P, P], F32, name="identity")
         make_identity(nc, identity[:])
@@ -87,16 +87,16 @@ def tile_picked_ahzmthesndpagsn_none_po_kernel(tc, x_words, x_scales, d_words, d
         def mx(acc, cols, cols_scale, rows, rows_scale, start, stop):
             nc.tensor.matmul_mx(acc, lhsT=cols.bitcast(FP8X4), lhsT_scale=cols_scale, rhs=rows.bitcast(FP8X4), rhs_scale=rows_scale, start=start, stop=stop)
 
-        picked1 = keep.tile([P, H + S], U8, name="picked1")
+        picked1 = keep.tile([P, H + S], U8, name="picked1", tag="picked")
         picked_b = keep.tile([P, H], U8, name="picked_b")
-        gather(picked1[:, 0:H], d_bytes, l_ka[:])
         gather(picked1[:, H:], x_bytes, l_offs[:])
+        gather(picked1[:, 0:H], d_bytes, l_ka[:])
         move_rows(plane1, picked1)
         gather(picked_b[:], d_bytes, l_kb[:])
         move_rows(plane_b, picked_b)
 
         xq = keep.tile([P, S], U32, name="xq", align_bytes=64)
-        wa = keep.tile([P, H], U32, name="wa", tag="first", align_bytes=64)
+        wa = keep.tile([P, H], U32, name="wa", align_bytes=64)
         wb = keep.tile([P, H], U32, name="wb", align_bytes=64)
         gather(xq[:], x_table, l_offs[:])
         gather(wa[:], d_table, l_ka[:])
@@ -143,7 +143,7 @@ def tile_picked_ahzmthesndpagsn_none_po_kernel(tc, x_words, x_scales, d_words, d
                 gate(sg0, t, 0)
             nc.scalar.activation(ds[t][:].indirect(l_n1[:]), h[t][:], ACT.Copy)
 
-        picked2 = keep.tile([P, 3 * H + 2 * S], U8, name="picked2", tag="first", align_bytes=64)
+        picked2 = keep.tile([P, 3 * H + 2 * S], U8, name="picked2", tag="picked")
         gather(picked2[:, 0:H], d_bytes, l_k2[:])
         gather(picked2[:, H : 2 * H], d_bytes, l_k3[:])
         gather(picked2[:, 2 * H : 3 * H], d_bytes, l_k1[:])

@@ -48,8 +48,14 @@ def tile_picked_ahzmthesndpagsn_none_po_kernel(tc, x_words, x_scales, d_words, d
         l_kb = load_list("kb", kb)
         x_table = keep.tile([P, T], U32, name="x_table")
         d_table = keep.tile([P, G], U32, name="d_table")
-        nc.sync.dma_start(x_table[:].bitcast(I32), x_words[0].rearrange("p c r -> p (c r)").bitcast(I32))
+        slope = keep.tile([P, PACK], F32, name="slope")
+        thresh = keep.tile([P, PACK], F32, name="thresh")
+        gain = keep.tile([P, PACK], F32, name="gain")
         nc.gpsimd.dma_start(d_table[:].bitcast(I32), d_words[0].rearrange("p c r -> p (c r)").bitcast(I32))
+        nc.gpsimd.dma_start(slope[:], sl.rearrange("(p t) o -> p (t o)", t=PACK))
+        nc.gpsimd.dma_start(x_table[:].bitcast(I32), x_words[0].rearrange("p c r -> p (c r)").bitcast(I32))
+        identity = keep.tile([P, P], F32, name="identity")
+        make_identity(nc, identity[:])
         l_n1 = load_list("n1", n1)
         l_n2 = load_list("n2", n2)
         l_k2 = load_list("k2", k2)
@@ -61,10 +67,7 @@ def tile_picked_ahzmthesndpagsn_none_po_kernel(tc, x_words, x_scales, d_words, d
         l_n3 = load_list("n3", n3)
         l_n4 = load_list("n4", n4)
 
-        slope = keep.tile([P, PACK], F32, name="slope")
-        thresh = keep.tile([P, PACK], F32, name="thresh")
-        gain = keep.tile([P, PACK], F32, name="gain")
-        for tile, dram in ((slope, sl), (thresh, th), (gain, gs)):
+        for tile, dram in ((thresh, th), (gain, gs)):
             nc.gpsimd.dma_start(tile[:], dram.rearrange("(p t) o -> p (t o)", t=PACK))
 
         plane1 = keep.tile([P, H + S], U8, name="plane1", align_bytes=64)
@@ -81,9 +84,6 @@ def tile_picked_ahzmthesndpagsn_none_po_kernel(tc, x_words, x_scales, d_words, d
             for q in range(4):
                 nc.sync.dma_start(plane[32 * q : 32 * q + 4, :].bitcast(I32), picked[32 * q : 32 * (q + 1) : 8, :].bitcast(I32))
 
-        identity = keep.tile([P, P], F32, name="identity")
-        make_identity(nc, identity[:])
-
         def mx(acc, cols, cols_scale, rows, rows_scale, start, stop):
             nc.tensor.matmul_mx(acc, lhsT=cols.bitcast(FP8X4), lhsT_scale=cols_scale, rhs=rows.bitcast(FP8X4), rhs_scale=rows_scale, start=start, stop=stop)
 
@@ -98,8 +98,8 @@ def tile_picked_ahzmthesndpagsn_none_po_kernel(tc, x_words, x_scales, d_words, d
         xq = keep.tile([P, S], U32, name="xq", align_bytes=64)
         wa = keep.tile([P, H], U32, name="wa", align_bytes=64)
         wb = keep.tile([P, H], U32, name="wb", align_bytes=64)
-        gather(xq[:], x_table, l_offs[:])
         gather(wa[:], d_table, l_ka[:])
+        gather(xq[:], x_table, l_offs[:])
         for v in range(2):
             gather(wb[:, v * H // 2 : (v + 1) * H // 2], d_table, l_kb[:, 16 * v : 16 * (v + 1)])
 
@@ -120,7 +120,7 @@ def tile_picked_ahzmthesndpagsn_none_po_kernel(tc, x_words, x_scales, d_words, d
             nc.scalar.activation(sg[:, t, :], h[t][:].indirect(l_n2[:, 8 * u : 8 * (u + 1)]), ACT.Sigmoid, scale=slope[:, t : t + 1], bias=bias[:, t : t + 1])
 
         sg0 = keep.tile([P, PACK, HALF], F32, name="sg0", tag="sg")
-        late = [keep.tile([P, 2, P], F32, name=f"late{u}") for u in range(2)]
+        late = [keep.tile([P, 2, P], F32, name=f"late{u}", tag=f"late{u}", align_bytes=64) for u in range(2)]
         for t in range(PACK):
             turned = psum.tile([P, S], F32, name=f"turned{t}", tag=f"turn{t}")
             for u in range(2):
@@ -136,7 +136,10 @@ def tile_picked_ahzmthesndpagsn_none_po_kernel(tc, x_words, x_scales, d_words, d
                 nc.tensor.transpose(turned[:, u * HALF : (u + 1) * HALF], src, identity[:])
             h.append(keep.tile([P, S], F32, name=f"h{t}"))
             ds.append(keep.tile([P, DS_WIDTH], F32, name=f"ds{t}"))
-            nc.scalar.activation(h[t][:], turned[:], ACT.Copy, scale=0.0625)
+            if t < 2:
+                nc.scalar.activation(h[t][:], turned[:], ACT.Copy, scale=0.0625)
+            else:
+                nc.vector.tensor_scalar(h[t][:], turned[:], 0.0625, None, ALU.mult)
             if t > 0:
                 gate(sg0, t - 1, 0)
             if t == PACK - 1:
@@ -150,7 +153,7 @@ def tile_picked_ahzmthesndpagsn_none_po_kernel(tc, x_words, x_scales, d_words, d
         gather(picked2[:, 3 * H : 3 * H + S], x_bytes, l_two[:])
         gather(picked2[:, 3 * H + S :], x_bytes, l_hz[:])
         move_rows(plane2, picked2)
-        words2 = keep.tile([P, 3 * H + 2 * S], U32, name="words2", tag="early1_1", align_bytes=64)
+        words2 = keep.tile([P, 3 * H + 2 * S], U32, name="words2", tag="late1", align_bytes=64)
         gather(words2[:, 3 * H : 3 * H + S], x_table, l_two[:])
         gather(words2[:, 0:H], d_table, l_k2[:])
         gather(words2[:, 3 * H + S :], x_table, l_hz[:])

from contextlib import ExitStack

import concourse.mybir as mybir
from concourse.masks import make_identity

K, T, S, G, H, U = 512, 1024, 256, 2048, 512, 512
FLOPS = 5 * 2 * K * H * S

F32 = mybir.dt.float32
BF16 = mybir.dt.bfloat16
I32 = mybir.dt.int32
U32 = mybir.dt.uint32
U16 = mybir.dt.uint16
U8 = mybir.dt.uint8
FP8X4 = mybir.dt.float8_e4m3fn_x4
ACT = mybir.ActivationFunctionType
ALU = mybir.AluOpType

P = 128
PACK = 4
HALF = S // 2
DS_WIDTH = 352


def tile_picked_ahzmthesndpagsn_none_po_kernel(tc, x_words, x_scales, d_words, d_scales, sl, th, gs, offs, ka, kb, n1, n2, k1, k2, two, k3, hz, n3, n4, n5, out_0, out_1, out_2):
    nc = tc.nc
    with ExitStack() as ctx:
        lists = ctx.enter_context(tc.tile_pool(name="lists", bufs=1))
        keep = ctx.enter_context(tc.tile_pool(name="keep", bufs=1))
        psum = ctx.enter_context(tc.psum_pool(name="psum", bufs=1))

        def load_list(name, dram):
            tile = lists.tile(list(dram.shape), U16, name="list_" + name)
            nc.sync.dma_start(tile[:], dram)
            return tile

        d_bytes = keep.tile([P, G], U8, name="d_bytes")
        x_bytes = keep.tile([P, T], U8, name="x_bytes")
        for tile, dram in ((x_bytes, x_scales), (d_bytes, d_scales)):
            rows = dram[0].bitcast(I32)
            nc.scalar.dma_start(tile[:].bitcast(I32), rows.unsqueeze(1).to_broadcast([16, 8, rows.shape[1]]))

        warm = keep.tile([P, 2], F32, name="warm")
        nc.vector.memset(warm[:, 0:1], 0.0)
        nc.scalar.activation(warm[:, 1:2], warm[:, 0:1], ACT.Sigmoid)
        l_offs = load_list("offs", offs)
        l_ka = load_list("ka", ka)
        l_kb = load_list("kb", kb)
        x_table = keep.tile([P, T], U32, name="x_table")
        d_table = keep.tile([P, G], U32, name="d_table")
        slope = keep.tile([P, PACK], F32, name="slope")
        thresh = keep.tile([P, PACK], F32, name="thresh")
        gain = keep.tile([P, PACK], F32, name="gain")
        nc.gpsimd.dma_start(d_table[:].bitcast(I32), d_words[0].rearrange("p c r -> p (c r)").bitcast(I32))
        nc.gpsimd.dma_start(slope[:], sl.rearrange("(p t) o -> p (t o)", t=PACK))
        nc.gpsimd.dma_start(x_table[:].bitcast(I32), x_words[0].rearrange("p c r -> p (c r)").bitcast(I32))
        identity = keep.tile([P, P], F32, name="identity")
        make_identity(nc, identity[:])
        l_n1 = load_list("n1", n1)
        l_n2 = load_list("n2", n2)
        l_k2 = load_list("k2", k2)
        l_k3 = load_list("k3", k3)
        l_k1 = load_list("k1", k1)
        l_two = load_list("two", two)
        l_hz = load_list("hz", hz)
        l_n5 = load_list("n5", n5)
        l_n3 = load_list("n3", n3)
        l_n4 = load_list("n4", n4)

        for tile, dram in ((thresh, th), (gain, gs)):
            nc.gpsimd.dma_start(tile[:], dram.rearrange("(p t) o -> p (t o)", t=PACK))

        plane1 = keep.tile([P, H + S], U8, name="plane1", align_bytes=64)
        plane_b = keep.tile([P, H], U8, name="plane_b", align_bytes=64)
        plane2 = keep.tile([P, 3 * H + 2 * S], U8, name="plane2", align_bytes=64)
        nc.vector.memset(plane1[:].bitcast(I32), 0)
        nc.vector.memset(plane_b[:].bitcast(I32), 0)
        nc.vector.memset(plane2[:].bitcast(I32), 0)

        def gather(dst, table, offsets):
            nc.vector.tensor_copy(dst, table[:].indirect(offsets))

        def move_rows(plane, picked):
            for q in range(4):
                nc.sync.dma_start(plane[32 * q : 32 * q + 4, :].bitcast(I32), picked[32 * q : 32 * (q + 1) : 8, :].bitcast(I32))

        def mx(acc, cols, cols_scale, rows, rows_scale, start, stop):
            nc.tensor.matmul_mx(acc, lhsT=cols.bitcast(FP8X4), lhsT_scale=cols_scale, rhs=rows.bitcast(FP8X4), rhs_scale=rows_scale, start=start, stop=stop)

        picked1 = keep.tile([P, H + S], U8, name="picked1", tag="picked")
        picked_b = keep.tile([P, H], U8, name="picked_b")
        gather(picked1[:, H:], x_bytes, l_offs[:])
        gather(picked1[:, 0:H], d_bytes, l_ka[:])
        move_rows(plane1, picked1)
        gather(picked_b[:], d_bytes, l_kb[:])
        move_rows(plane_b, picked_b)

        xq = keep.tile([P, S], U32, name="xq", align_bytes=64)
        wa = keep.tile([P, H], U32, name="wa", align_bytes=64)
        wb = keep.tile([P, H], U32, name="wb", align_bytes=64)
        gather(wa[:], d_table, l_ka[:])
        gather(xq[:], x_table, l_offs[:])
        for v in range(2):
            gather(wb[:, v * H // 2 : (v + 1) * H // 2], d_table, l_kb[:, 16 * v : 16 * (v + 1)])

        bias = keep.tile([P, PACK], F32, name="bias")
        product = keep.tile([P, PACK], F32, name="product")
        nc.gpsimd.tensor_tensor(product[:], slope[:], thresh[:], ALU.mult)
        nc.gpsimd.tensor_scalar(bias[:], product[:], -1.0, 0.0, ALU.mult, ALU.add)

        acc1 = [psum.tile([P, H], F32, name=f"acc1_{u}") for u in range(2)]
        for first, n, words, plane in ((0, H, wa, plane1), (0, H // 2, wb, plane_b), (H // 2, H // 2, wb, plane_b)):
            for u in range(2):
                rows = slice(first, first + n)
                mx(acc1[u][:, rows], xq[:, u * HALF : (u + 1) * HALF], plane1[:, H + u * HALF : H + (u + 1) * HALF], words[:, rows], plane[:, rows], n == H, first > 0)

        h, ds = [], []

        def gate(sg, t, u):
            nc.scalar.activation(sg[:, t, :], h[t][:].indirect(l_n2[:, 8 * u : 8 * (u + 1)]), ACT.Sigmoid, scale=slope[:, t : t + 1], bias=bias[:, t : t + 1])

        sg0 = keep.tile([P, PACK, HALF], F32, name="sg0", tag="sg")
        late = [keep.tile([P, 2, P], F32, name=f"late{u}", tag=f"late{u}", align_bytes=64) for u in range(2)]
        for t in range(PACK):
            turned = psum.tile([P, S], F32, name=f"turned{t}", tag=f"turn{t}")
            for u in range(2):
                dealt = acc1[u][:].rearrange("j (p t) -> j t p", t=PACK)
                if t < 2:
                    early = keep.tile([P, P], F32, name=f"early{u}_{t}", tag=f"early{u}_{t}", align_bytes=64)
                    nc.scalar.copy(early[:], dealt[:, t, :])
                    src = early[:]
                else:
                    if t == 2:
                        nc.vector.tensor_copy(late[u][:], dealt[:, 2:4, :])
                    src = late[u][:, t - 2, :]
                nc.tensor.transpose(turned[:, u * HALF : (u + 1) * HALF], src, identity[:])
            h.append(keep.tile([P, S], F32, name=f"h{t}"))
            ds.append(keep.tile([P, DS_WIDTH], F32, name=f"ds{t}"))
            if t < 2:
                nc.scalar.activation(h[t][:], turned[:], ACT.Copy, scale=0.0625)
            else:
                nc.vector.tensor_scalar(h[t][:], turned[:], 0.0625, None, ALU.mult)
            if t > 0:
                gate(sg0, t - 1, 0)
            if t == PACK - 1:
                gate(sg0, t, 0)
            nc.scalar.activation(ds[t][:].indirect(l_n1[:]), h[t][:], ACT.Copy)

        picked2 = keep.tile([P, 3 * H + 2 * S], U8, name="picked2", tag="picked")
        gather(picked2[:, 0:H], d_bytes, l_k2[:])
        gather(picked2[:, H : 2 * H], d_bytes, l_k3[:])
        gather(picked2[:, 2 * H : 3 * H], d_bytes, l_k1[:])
        gather(picked2[:, 3 * H : 3 * H + S], x_bytes, l_two[:])
        gather(picked2[:, 3 * H + S :], x_bytes, l_hz[:])
        move_rows(plane2, picked2)
        words2 = keep.tile([P, 3 * H + 2 * S], U32, name="words2", tag="late1", align_bytes=64)
        gather(words2[:, 3 * H : 3 * H + S], x_table, l_two[:])
        gather(words2[:, 0:H], d_table, l_k2[:])
        gather(words2[:, 3 * H + S :], x_table, l_hz[:])
        gather(words2[:, H : 2 * H], d_table, l_k3[:])
        gather(words2[:, 2 * H : 3 * H], d_table, l_k1[:])

        acc2 = [psum.tile([P, H], F32, name=f"acc2_{u}") for u in range(2)]
        for l in range(2):
            for u in range(2):
                x_cols = slice(3 * H + l * S + u * HALF, 3 * H + l * S + (u + 1) * HALF)
                d_cols = slice(l * H, (l + 1) * H)
                mx(acc2[u][:], words2[:, x_cols], plane2[:, x_cols], words2[:, d_cols], plane2[:, d_cols], l == 0, False)

        h2 = [keep.tile([P, S], F32, name=f"h2_{t}") for t in range(PACK)]
        ds2 = [keep.tile([P, S], F32, name=f"ds2_{t}") for t in range(PACK)]
        up = [keep.tile([P, S], F32, name=f"up{t}") for t in range(PACK)]
        for u in range(2):
            cols = slice(u * HALF, (u + 1) * HALF)
            if u == 0:
                sg = sg0
            else:
                sg = keep.tile([P, PACK, HALF], F32, name="sg1", tag="sg")
                for t in range(PACK):
                    gate(sg, t, u)
            z_planes = keep.tile([P, PACK, HALF], BF16, name=f"z_planes{u}", tag=("z_planes", "z_words")[u], align_bytes=64)
            z_words = keep.tile([P, HALF, PACK], BF16, name=f"z_words{u}", tag=("z_words", "rows0_0")[u], align_bytes=64)
            z_codes = keep.tile([P, HALF], U32, name=f"z_codes{u}", align_bytes=64)
            z_scales = keep.tile([P, HALF], U8, name=f"z_scales{u}", align_bytes=64)
            for t in range(PACK):
                nc.vector.scalar_tensor_tensor(z_planes[:, t, :], ds[t][:, cols], gain[:, t : t + 1], sg[:, t, :], ALU.mult, ALU.mult)
            nc.vector.tensor_copy(z_words[:], z_planes[:].rearrange("p t c -> p c t"))
            nc.vector.quantize_mx(out=z_codes[:].bitcast(FP8X4), scales=z_scales[:], in_=z_words[:].rearrange("p c t -> p (c t)"))
            d_cols = slice(2 * H, 3 * H)
            mx(acc2[u][:], z_codes[:], z_scales[:], words2[:, d_cols], plane2[:, d_cols], False, True)
            dealt = acc2[u][:].rearrange("j (p t) -> j t p", t=PACK)
            for t in range(PACK):
                rows = keep.tile([P, P], F32, name=f"rows{u}_{t}", tag=f"rows{u}_{t}", align_bytes=64)
                nc.vector.tensor_copy(rows[:], dealt[:, t, :])
                turned = psum.tile([P, HALF], F32, name=f"turned2_{u}_{t}", tag=f"turn{t}")
                nc.tensor.transpose(turned[:], rows[:], identity[:])
                nc.vector.tensor_scalar(h2[t][:, cols], turned[:], 0.0625, None, ALU.mult)
                if u == 0:
                    nc.scalar.activation(ds2[t][:].indirect(l_n5[:, 0:8]), h2[t][:, cols], ACT.Copy)

        page = [keep.tile([P, U], F32, name=f"page{t}", tag=f"rows1_{t}", align_bytes=64) for t in range(PACK)]
        for t in range(PACK):
            nc.vector.memset(page[t][:], 0.0)
        y_words = [keep.tile([P, U // 2, PACK], BF16, name=f"y_words{u}", align_bytes=64) for u in range(2)]
        y_codes = keep.tile([P, U], U32, name="y_codes", align_bytes=64)
        y_scales = keep.tile([P, U], U8, name="y_scales", align_bytes=64)
        out_rows = out_0.rearrange("(p t) c -> p t c", t=PACK)

        def finish_ds2(t):
            nc.scalar.activation(ds2[t][:].indirect(l_n5[:, 8:16]), h2[t][:, HALF:], ACT.Copy)
            nc.vector.tensor_tensor(up[t][:], h2[t][:], ds2[t][:], ALU.max)

        finish_ds2(0)
        for t in range(PACK):
            if t + 1 < PACK:
                finish_ds2(t + 1)
            nc.scalar.activation(page[t][:].indirect(l_n3[:]), ds2[t][:], ACT.Copy)
            if t > 0:
                finish_page(nc, t - 1, page, l_n4, up, y_words, out_rows, nc.sync)
        finish_page(nc, PACK - 1, page, l_n4, up, y_words, out_rows, nc.scalar)

        codes_out = out_1[0].rearrange("p c r -> p (c r)").bitcast(I32)
        for u in range(2):
            cols = slice(u * U // 2, (u + 1) * U // 2)
            nc.vector.quantize_mx(out=y_codes[:, cols].bitcast(FP8X4), scales=y_scales[:, cols], in_=y_words[u][:].rearrange("p c t -> p (c t)"))
            nc.sync.dma_start(codes_out[:, cols], y_codes[:, cols].bitcast(I32))
        for q in range(4):
            (nc.scalar, nc.sync)[q % 2].dma_start(out_2[0][4 * q : 4 * q + 4, :].bitcast(I32), y_scales[32 * q : 32 * q + 4, :].bitcast(I32))


def finish_page(nc, t, page, l_n4, up, y_words, out_rows, queue):
    nc.scalar.activation(page[t][:].indirect(l_n4[:]), up[t][:], ACT.Copy)
    queue.dma_start(out_rows[:, t, :], page[t][:])
    for u in range(2):
        nc.vector.tensor_copy(y_words[u][:, :, t], page[t][:, u * U // 2 : (u + 1) * U // 2])
